import numpy as np
CORES = [4,5,6,7,12,13,14,15,20,21,22,23,28,29,30,31,36,37,38,39,44,45,46,47]
N = 24
WIDTHS = [2,9,16,23,30,37,44,51,58,2,9,16,23,30,37,44,51,58,2,9,16,23,30,37]
XW = 58
def setup_inputs(rng):
    return {"x": rng.standard_normal((N, 128, XW), dtype=np.float32)}
def reference(x):
    g = np.concatenate([x[r][:, :WIDTHS[r]] for r in range(N)], axis=1)
    return {"y": np.broadcast_to(g, (N,) + g.shape)}

@@ -1,0 +1,203 @@
+import concourse.bass as bass
+
+TOTAL = 657
+SCRATCH = {"land": ("sbuf", [128, TOTAL], "float32")}
+SEMAPHORES = ["loaded", "stored", "sent", "g", "c", "f"]
+CFG = {"design": "V1", "frac": 0.0, "die1": True}
+
+ALL16 = 0xFFFF
+LOW8 = 0x00FF
+HIGH8 = 0xFF00
+
+
+def popcount(m):
+    return bin(m).count("1")
+
+
+def build(widths, cores, topo, cfg):
+    design = cfg["design"]
+    off = [0]
+    for w in widths:
+        off.append(off[-1] + w)
+    prog = {}
+    tot = {}
+
+    def emit(core, op):
+        prog.setdefault(core, []).append(op)
+
+    def bump(core, sem, n):
+        tot[(core, sem)] = tot.get((core, sem), 0) + n
+
+    def send(src, transfers):
+        emit(src, ("send", transfers))
+        for lo, hi, dsts, mask, sem in transfers:
+            bump(src, "sent", popcount(mask))
+            for d in dsts:
+                bump(d, sem, popcount(mask))
+
+    nchip = len(cores) // 4
+    rk = [[cores[4 * c + i] for i in range(4)] for c in range(nchip)]
+    hp = [[8 * c + i for i in range(4)] for c in range(nchip)]
+    blk = [(off[4 * c], off[4 * c + 4]) for c in range(nchip)]
+    pc = [[(off[4 * c + i], off[4 * c + i + 1]) for i in range(4)] for c in range(nchip)]
+
+    for c in range(nchip):
+        for i in range(4):
+            emit(rk[c][i], ("load", pc[c][i][0], pc[c][i][1]))
+
+    if design == "V1":
+        die1 = cfg["die1"]
+        mid = [(blk[c][0] + blk[c][1] + 1) // 2 for c in range(nchip)]
+        for c in range(nchip):
+            for i in range(4):
+                lo, hi = pc[c][i]
+                dsts = []
+                if die1:
+                    dsts += [hp[c][0], hp[c][2]]
+                    if lo < mid[c]:
+                        dsts.append(hp[c][3])
+                dsts += [rk[c][j] for j in (0, 2, 3, 1) if j != i]
+                send(rk[c][i], [(lo, hi, dsts, ALL16, "g")])
+        recv = {}
+        for d in range(nchip):
+            srcs = [s for s in range(nchip) if s != d and s != (d ^ 1)]
+            srcs.sort(key=lambda s: -(blk[s][1] - blk[s][0]))
+            for s, k in zip(srcs, (1, 0, 2, 3)):
+                recv[(s, d)] = rk[d][k]
+        fwd = []
+        late = []
+        for c in range(nchip):
+            m = c ^ 1
+            lo, hi = blk[c]
+            if die1:
+                flows = [(rk[c][0], (c + 2) % nchip, lo, hi, None), (rk[c][2], (m + 2) % nchip, lo, hi, None),
+                         (hp[c][0], (c + 4) % nchip, lo, hi, None), (hp[c][2], (m + 4) % nchip, lo, hi, None),
+                         (rk[c][3], m, mid[c], hi, hp[m][1]), (hp[c][3], m, lo, mid[c], hp[m][0])]
+            else:
+                flows = [(rk[c][0], (c + 2) % nchip, lo, hi, None), (rk[c][2], (m + 2) % nchip, lo, hi, None),
+                         (rk[c][1], (c + 4) % nchip, lo, hi, None), (rk[c][3], (m + 4) % nchip, lo, hi, None),
+                         (rk[c][2], m, mid[c], hi, hp[m][1]), (rk[c][3], m, lo, mid[c], hp[m][0])]
+            for src, d, a, b, r in flows:
+                emit(src, ("wait", "g"))
+                if r is None:
+                    r = recv[(c, d)]
+                s = b - int(round(cfg["frac"] * (b - a)))
+                send(src, [(a, s, [r], LOW8, "c")])
+                fwd.append((r, d, a, s))
+                if s < b:
+                    late.append((src, d, s, b))
+        for src, d, a, b in late:
+            send(src, [(a, b, list(rk[d]), LOW8, "f")])
+        for r, d, a, b in fwd:
+            emit(r, ("wait", "c"))
+            send(r, [(a, b, [q for q in rk[d] if q != r], ALL16, "f")])
+
+    elif design == "V2":
+        for c in range(nchip):
+            for i in range(4):
+                lo, hi = pc[c][i]
+                dsts = list(hp[c]) + [rk[c][j] for j in range(4) if j != i]
+                send(rk[c][i], [(lo, hi, dsts, ALL16, "g")])
+        for c in range(nchip):
+            m = c ^ 1
+            lo, hi = blk[c]
+            for side, same, other, mt in ((rk[c], (c + 2) % nchip, (m + 2) % nchip, (0, 1)),
+                                          (hp[c], (c + 4) % nchip, (m + 4) % nchip, (2, 3))):
+                jobs = [(side[0], rk[same][0:2]), (side[1], rk[same][2:4]), (side[2], rk[other][0:3]),
+                        (side[3], [rk[other][3], rk[m][mt[0]], rk[m][mt[1]]])]
+                for src, dsts in jobs:
+                    emit(src, ("wait", "g"))
+                    send(src, [(lo, hi, list(dsts), LOW8, "f")])
+
+    elif design == "Q":
+        h45 = [(pc[c][0][0], pc[c][1][1]) for c in range(nchip)]
+        h67 = [(pc[c][2][0], pc[c][3][1]) for c in range(nchip)]
+        job = {}
+        for d in range(nchip):
+            plane = [s for s in range(nchip) if (s & 1) == (d & 1)]
+            plane.sort(key=lambda s: -(h45[s][1] - h45[s][0]))
+            for s, k in zip(plane, (hp[d][2], rk[d][2], rk[d][3])):
+                job[(s, 45, d)] = k
+            rest = [s for s in range(nchip) if s != d]
+            rest.sort(key=lambda s: -(h67[s][1] - h67[s][0]))
+            for s, k in zip(rest, (rk[d][0], rk[d][1], hp[d][0], hp[d][1], hp[d][3])):
+                job[(s, 67, d)] = k
+        for c in range(nchip):
+            m = c ^ 1
+            for i in range(4):
+                lo, hi = pc[c][i]
+                me = rk[c][i]
+                on_g = [rk[c][j] for j in range(4) if j != i]
+                tr = [(lo, hi, on_g, HIGH8, "g")]
+                offc = []
+                half = 45 if i < 2 else 67
+                for d in ((c + 2) % nchip, (c + 4) % nchip):
+                    offc.append(job[(c, half, d)])
+                if i >= 2:
+                    for d in (m, (m + 2) % nchip, (m + 4) % nchip):
+                        offc.append(job[(c, 67, d)])
+                z = job[(c, 45, c)]
+                if i < 2 and z not in rk[c]:
+                    tr = [(lo, hi, on_g, 0x0F00, "g"), (lo, hi, [z], 0xF000, "c")]
+                tr.append((lo, hi, offc, LOW8, "c"))
+                send(me, tr)
+        for d in range(nchip):
+            m = d ^ 1
+            for (s, half, dd), k in sorted(job.items()):
+                if dd != d:
+                    continue
+                a, b = h45[s] if half == 45 else h67[s]
+                on = [q for q in rk[d] if q != k]
+                if s == d:
+                    emit(k, ("wait", "g" if k in rk[d] else "c"))
+                    send(k, [(a, b, list(rk[m]), LOW8, "f")])
+                elif half == 45:
+                    emit(k, ("wait", "c"))
+                    send(k, [(a, b, on, HIGH8, "f"), (a, b, list(rk[m]), LOW8, "f")])
+                else:
+                    emit(k, ("wait", "c"))
+                    send(k, [(a, b, on, ALL16, "f")])
+
+    for c in range(nchip):
+        for q in rk[c]:
+            for s in ("g", "c", "f"):
+                if (q, s) in tot:
+                    emit(q, ("wait", s))
+            emit(q, ("store", 0, off[-1]))
+        for q in rk[c] + hp[c]:
+            if (q, "sent") in tot:
+                emit(q, ("wait", "sent"))
+    return prog, tot
+
+
+def rank_program(g, core, T, topo):
+    prog, tot = build(list(T.tables["WIDTHS"]), list(T.cores), topo, CFG)
+    sems = {"sent": T.sem.sent, "g": T.sem.g, "c": T.sem.c, "f": T.sem.f}
+    land = T.land
+    done = set()
+    nstore = 0
+    for op in prog.get(core, []):
+        if op[0] == "load":
+            lo, hi = op[1], op[2]
+            g.dma_start(land[:, lo:hi], T.x[:, 0:hi - lo]).then_inc(T.sem.loaded, 16)
+            g.wait_ge(T.sem.loaded, 16)
+        elif op[0] == "wait":
+            if op[1] not in done:
+                done.add(op[1])
+                g.wait_ge(sems[op[1]], tot[(core, op[1])])
+        elif op[0] == "send":
+            trs = []
+            for lo, hi, dsts, mask, sem in op[1]:
+                ids = []
+                for d in dsts:
+                    rid, pid, se = topo.addr(d)
+                    ids.append(bass.DstId(rid=rid, pnc=pid))
+                trs.append(bass.RemoteDMATransfer(dst_ids=ids, dma_engine_mask=mask, remote_sem=sems[sem],
+                                                  srcs=[land[:, lo:hi]], dsts=[land[:, lo:hi] for d in dsts]))
+            g.remote_dma_fused(trs, local_sem=T.sem.sent)
+        elif op[0] == "store":
+            lo, hi = op[1], op[2]
+            g.dma_start(T.y[:, lo:hi], land[:, lo:hi]).then_inc(T.sem.stored, 16)
+            nstore += 16
+    if nstore:
+        g.wait_ge(T.sem.stored, nstore)

@@ -2,8 +2,7 @@ import concourse.bass as bass
 
 TOTAL = 657
 SCRATCH = {"land": ("sbuf", [128, TOTAL], "float32")}
-SEMAPHORES = ["loaded", "stored", "sent", "g", "c", "f"]
-CFG = {"design": "V1", "frac": 0.0, "die1": True}
+SEMAPHORES = ["loaded", "stored", "sent", "g", "r", "c", "b", "f"]
 
 ALL16 = 0xFFFF
 LOW8 = 0x00FF
@@ -14,8 +13,7 @@ def popcount(m):
     return bin(m).count("1")
 
 
-def build(widths, cores, topo, cfg):
-    design = cfg["design"]
+def build(widths, cores, topo):
     off = [0]
     for w in widths:
         off.append(off[-1] + w)
@@ -35,132 +33,66 @@ def build(widths, cores, topo, cfg):
             for d in dsts:
                 bump(d, sem, popcount(mask))
 
+    def width(ab):
+        return ab[1] - ab[0]
+
     nchip = len(cores) // 4
     rk = [[cores[4 * c + i] for i in range(4)] for c in range(nchip)]
     hp = [[8 * c + i for i in range(4)] for c in range(nchip)]
-    blk = [(off[4 * c], off[4 * c + 4]) for c in range(nchip)]
     pc = [[(off[4 * c + i], off[4 * c + i + 1]) for i in range(4)] for c in range(nchip)]
+    blk = [(off[4 * c], off[4 * c + 4]) for c in range(nchip)]
+    h45 = [(pc[c][0][0], pc[c][1][1]) for c in range(nchip)]
+    h67 = [(pc[c][2][0], pc[c][3][1]) for c in range(nchip)]
 
     for c in range(nchip):
         for i in range(4):
             emit(rk[c][i], ("load", pc[c][i][0], pc[c][i][1]))
 
-    if design == "V1":
-        die1 = cfg["die1"]
-        mid = [(blk[c][0] + blk[c][1] + 1) // 2 for c in range(nchip)]
-        for c in range(nchip):
-            for i in range(4):
-                lo, hi = pc[c][i]
-                dsts = []
-                if die1:
-                    dsts += [hp[c][0], hp[c][2]]
-                    if lo < mid[c]:
-                        dsts.append(hp[c][3])
-                dsts += [rk[c][j] for j in (0, 2, 3, 1) if j != i]
-                send(rk[c][i], [(lo, hi, dsts, ALL16, "g")])
-        recv = {}
-        for d in range(nchip):
-            srcs = [s for s in range(nchip) if s != d and s != (d ^ 1)]
-            srcs.sort(key=lambda s: -(blk[s][1] - blk[s][0]))
-            for s, k in zip(srcs, (1, 0, 2, 3)):
-                recv[(s, d)] = rk[d][k]
-        fwd = []
-        late = []
-        for c in range(nchip):
-            m = c ^ 1
-            lo, hi = blk[c]
-            if die1:
-                flows = [(rk[c][0], (c + 2) % nchip, lo, hi, None), (rk[c][2], (m + 2) % nchip, lo, hi, None),
-                         (hp[c][0], (c + 4) % nchip, lo, hi, None), (hp[c][2], (m + 4) % nchip, lo, hi, None),
-                         (rk[c][3], m, mid[c], hi, hp[m][1]), (hp[c][3], m, lo, mid[c], hp[m][0])]
+    ajob, bjob, arange = {}, {}, {}
+    for d in range(nchip):
+        srcs = [s for s in range(nchip) if s != d]
+        for s in srcs:
+            arange[(s, d)] = blk[s] if (s & 1) == (d & 1) else h67[s]
+        srcs.sort(key=lambda s: -width(arange[(s, d)]))
+        for s, k in zip(srcs, (hp[d][0], hp[d][1], hp[d][3], hp[d][2], rk[d][2])):
+            ajob[(s, d)] = k
+        oth = [s for s in range(nchip) if (s & 1) != (d & 1)]
+        oth.sort(key=lambda s: -width(h45[s]))
+        for s, k in zip(oth, (rk[d][0], rk[d][1], rk[d][3])):
+            bjob[(s, d)] = k
+
+    for c in range(nchip):
+        m = c ^ 1
+        same = [(c + 2) % nchip, (c + 4) % nchip]
+        other = [m, (m + 2) % nchip, (m + 4) % nchip]
+        for i in range(4):
+            lo, hi = pc[c][i]
+            if i < 2:
+                send(rk[c][i], [(lo, hi, [hp[c][2], rk[c][2]], HIGH8, "r"),
+                                (lo, hi, [ajob[(c, d)] for d in same], 0x000F, "c"),
+                                (lo, hi, [rk[c][1 - i], rk[c][3]], 0x00F0, "g")])
             else:
-                flows = [(rk[c][0], (c + 2) % nchip, lo, hi, None), (rk[c][2], (m + 2) % nchip, lo, hi, None),
-                         (rk[c][1], (c + 4) % nchip, lo, hi, None), (rk[c][3], (m + 4) % nchip, lo, hi, None),
-                         (rk[c][2], m, mid[c], hi, hp[m][1]), (rk[c][3], m, lo, mid[c], hp[m][0])]
-            for src, d, a, b, r in flows:
-                emit(src, ("wait", "g"))
-                if r is None:
-                    r = recv[(c, d)]
-                s = b - int(round(cfg["frac"] * (b - a)))
-                send(src, [(a, s, [r], LOW8, "c")])
-                fwd.append((r, d, a, s))
-                if s < b:
-                    late.append((src, d, s, b))
-        for src, d, a, b in late:
-            send(src, [(a, b, list(rk[d]), LOW8, "f")])
-        for r, d, a, b in fwd:
-            emit(r, ("wait", "c"))
-            send(r, [(a, b, [q for q in rk[d] if q != r], ALL16, "f")])
-
-    elif design == "V2":
-        for c in range(nchip):
-            for i in range(4):
-                lo, hi = pc[c][i]
-                dsts = list(hp[c]) + [rk[c][j] for j in range(4) if j != i]
-                send(rk[c][i], [(lo, hi, dsts, ALL16, "g")])
-        for c in range(nchip):
-            m = c ^ 1
-            lo, hi = blk[c]
-            for side, same, other, mt in ((rk[c], (c + 2) % nchip, (m + 2) % nchip, (0, 1)),
-                                          (hp[c], (c + 4) % nchip, (m + 4) % nchip, (2, 3))):
-                jobs = [(side[0], rk[same][0:2]), (side[1], rk[same][2:4]), (side[2], rk[other][0:3]),
-                        (side[3], [rk[other][3], rk[m][mt[0]], rk[m][mt[1]]])]
-                for src, dsts in jobs:
-                    emit(src, ("wait", "g"))
-                    send(src, [(lo, hi, list(dsts), LOW8, "f")])
-
-    elif design == "Q":
-        h45 = [(pc[c][0][0], pc[c][1][1]) for c in range(nchip)]
-        h67 = [(pc[c][2][0], pc[c][3][1]) for c in range(nchip)]
-        job = {}
-        for d in range(nchip):
-            plane = [s for s in range(nchip) if (s & 1) == (d & 1)]
-            plane.sort(key=lambda s: -(h45[s][1] - h45[s][0]))
-            for s, k in zip(plane, (hp[d][2], rk[d][2], rk[d][3])):
-                job[(s, 45, d)] = k
-            rest = [s for s in range(nchip) if s != d]
-            rest.sort(key=lambda s: -(h67[s][1] - h67[s][0]))
-            for s, k in zip(rest, (rk[d][0], rk[d][1], hp[d][0], hp[d][1], hp[d][3])):
-                job[(s, 67, d)] = k
-        for c in range(nchip):
-            m = c ^ 1
-            for i in range(4):
-                lo, hi = pc[c][i]
-                me = rk[c][i]
-                on_g = [rk[c][j] for j in range(4) if j != i]
-                tr = [(lo, hi, on_g, HIGH8, "g")]
-                offc = []
-                half = 45 if i < 2 else 67
-                for d in ((c + 2) % nchip, (c + 4) % nchip):
-                    offc.append(job[(c, half, d)])
-                if i >= 2:
-                    for d in (m, (m + 2) % nchip, (m + 4) % nchip):
-                        offc.append(job[(c, 67, d)])
-                z = job[(c, 45, c)]
-                if i < 2 and z not in rk[c]:
-                    tr = [(lo, hi, on_g, 0x0F00, "g"), (lo, hi, [z], 0xF000, "c")]
-                tr.append((lo, hi, offc, LOW8, "c"))
-                send(me, tr)
-        for d in range(nchip):
-            m = d ^ 1
-            for (s, half, dd), k in sorted(job.items()):
-                if dd != d:
-                    continue
-                a, b = h45[s] if half == 45 else h67[s]
-                on = [q for q in rk[d] if q != k]
-                if s == d:
-                    emit(k, ("wait", "g" if k in rk[d] else "c"))
-                    send(k, [(a, b, list(rk[m]), LOW8, "f")])
-                elif half == 45:
-                    emit(k, ("wait", "c"))
-                    send(k, [(a, b, on, HIGH8, "f"), (a, b, list(rk[m]), LOW8, "f")])
-                else:
-                    emit(k, ("wait", "c"))
-                    send(k, [(a, b, on, ALL16, "f")])
+                send(rk[c][i], [(lo, hi, [ajob[(c, d)] for d in same + other], LOW8, "c"),
+                                (lo, hi, [rk[c][j] for j in range(4) if j != i], HIGH8, "g")])
+    for c in range(nchip):
+        m = c ^ 1
+        lo, hi = h45[c]
+        emit(hp[c][2], ("wait", "r"))
+        send(hp[c][2], [(lo, hi, [bjob[(c, (m + 2) % nchip)], bjob[(c, (m + 4) % nchip)]], LOW8, "b")])
+        emit(rk[c][2], ("wait", "r"))
+        send(rk[c][2], [(lo, hi, [bjob[(c, m)]], LOW8, "b")])
+    for (s, d), k in sorted(ajob.items()):
+        lo, hi = arange[(s, d)]
+        emit(k, ("wait", "c"))
+        send(k, [(lo, hi, [q for q in rk[d] if q != k], ALL16, "f")])
+    for (s, d), k in sorted(bjob.items()):
+        lo, hi = h45[s]
+        emit(k, ("wait", "b"))
+        send(k, [(lo, hi, [q for q in rk[d] if q != k], ALL16, "f")])
 
     for c in range(nchip):
         for q in rk[c]:
-            for s in ("g", "c", "f"):
+            for s in ("g", "r", "c", "b", "f"):
                 if (q, s) in tot:
                     emit(q, ("wait", s))
             emit(q, ("store", 0, off[-1]))
@@ -171,8 +103,8 @@ def build(widths, cores, topo, cfg):
 
 
 def rank_program(g, core, T, topo):
-    prog, tot = build(list(T.tables["WIDTHS"]), list(T.cores), topo, CFG)
-    sems = {"sent": T.sem.sent, "g": T.sem.g, "c": T.sem.c, "f": T.sem.f}
+    prog, tot = build(list(T.tables["WIDTHS"]), list(T.cores), topo)
+    sems = {"sent": T.sem.sent, "g": T.sem.g, "r": T.sem.r, "c": T.sem.c, "b": T.sem.b, "f": T.sem.f}
     land = T.land
     done = set()
     nstore = 0

@@ -68,19 +68,18 @@ def build(widths, cores, topo):
         for i in range(4):
             lo, hi = pc[c][i]
             if i < 2:
-                send(rk[c][i], [(lo, hi, [hp[c][2], rk[c][2]], HIGH8, "r"),
-                                (lo, hi, [ajob[(c, d)] for d in same], 0x000F, "c"),
-                                (lo, hi, [rk[c][1 - i], rk[c][3]], 0x00F0, "g")])
+                send(rk[c][i], [(lo, hi, [hp[c][2], hp[c][3], rk[c][2]], ALL16, "r")])
+                send(rk[c][i], [(lo, hi, [ajob[(c, d)] for d in same], LOW8, "c"),
+                                (lo, hi, [rk[c][1 - i], rk[c][3]], HIGH8, "g")])
             else:
                 send(rk[c][i], [(lo, hi, [ajob[(c, d)] for d in same + other], LOW8, "c"),
                                 (lo, hi, [rk[c][j] for j in range(4) if j != i], HIGH8, "g")])
     for c in range(nchip):
         m = c ^ 1
         lo, hi = h45[c]
-        emit(hp[c][2], ("wait", "r"))
-        send(hp[c][2], [(lo, hi, [bjob[(c, (m + 2) % nchip)], bjob[(c, (m + 4) % nchip)]], LOW8, "b")])
-        emit(rk[c][2], ("wait", "r"))
-        send(rk[c][2], [(lo, hi, [bjob[(c, m)]], LOW8, "b")])
+        for src, d in ((hp[c][2], (m + 2) % nchip), (hp[c][3], (m + 4) % nchip), (rk[c][2], m)):
+            emit(src, ("wait", "r"))
+            send(src, [(lo, hi, [bjob[(c, d)]], LOW8, "b")])
     for (s, d), k in sorted(ajob.items()):
         lo, hi = arange[(s, d)]
         emit(k, ("wait", "c"))

import concourse.bass as bass

TOTAL = 657
SCRATCH = {"land": ("sbuf", [128, TOTAL], "float32")}
SEMAPHORES = ["loaded", "stored", "sent", "g", "r", "c", "b", "f"]

ALL16 = 0xFFFF
LOW8 = 0x00FF
HIGH8 = 0xFF00


def popcount(m):
    return bin(m).count("1")


def build(widths, cores, topo):
    off = [0]
    for w in widths:
        off.append(off[-1] + w)
    prog = {}
    tot = {}

    def emit(core, op):
        prog.setdefault(core, []).append(op)

    def bump(core, sem, n):
        tot[(core, sem)] = tot.get((core, sem), 0) + n

    def send(src, transfers):
        emit(src, ("send", transfers))
        for lo, hi, dsts, mask, sem in transfers:
            bump(src, "sent", popcount(mask))
            for d in dsts:
                bump(d, sem, popcount(mask))

    def width(ab):
        return ab[1] - ab[0]

    nchip = len(cores) // 4
    rk = [[cores[4 * c + i] for i in range(4)] for c in range(nchip)]
    hp = [[8 * c + i for i in range(4)] for c in range(nchip)]
    pc = [[(off[4 * c + i], off[4 * c + i + 1]) for i in range(4)] for c in range(nchip)]
    blk = [(off[4 * c], off[4 * c + 4]) for c in range(nchip)]
    h45 = [(pc[c][0][0], pc[c][1][1]) for c in range(nchip)]
    h67 = [(pc[c][2][0], pc[c][3][1]) for c in range(nchip)]

    for c in range(nchip):
        for i in range(4):
            emit(rk[c][i], ("load", pc[c][i][0], pc[c][i][1]))

    ajob, bjob, arange = {}, {}, {}
    for d in range(nchip):
        srcs = [s for s in range(nchip) if s != d]
        for s in srcs:
            arange[(s, d)] = blk[s] if (s & 1) == (d & 1) else h67[s]
        srcs.sort(key=lambda s: -width(arange[(s, d)]))
        for s, k in zip(srcs, (hp[d][0], hp[d][1], hp[d][3], hp[d][2], rk[d][2])):
            ajob[(s, d)] = k
        oth = [s for s in range(nchip) if (s & 1) != (d & 1)]
        oth.sort(key=lambda s: -width(h45[s]))
        for s, k in zip(oth, (rk[d][0], rk[d][1], rk[d][3])):
            bjob[(s, d)] = k

    for c in range(nchip):
        m = c ^ 1
        same = [(c + 2) % nchip, (c + 4) % nchip]
        other = [m, (m + 2) % nchip, (m + 4) % nchip]
        for i in range(4):
            lo, hi = pc[c][i]
            if i < 2:
                send(rk[c][i], [(lo, hi, [hp[c][2], hp[c][3], rk[c][2]], ALL16, "r")])
                send(rk[c][i], [(lo, hi, [ajob[(c, d)] for d in same], LOW8, "c"),
                                (lo, hi, [rk[c][1 - i], rk[c][3]], HIGH8, "g")])
            else:
                send(rk[c][i], [(lo, hi, [ajob[(c, d)] for d in same + other], LOW8, "c"),
                                (lo, hi, [rk[c][j] for j in range(4) if j != i], HIGH8, "g")])
    for c in range(nchip):
        m = c ^ 1
        lo, hi = h45[c]
        for src, d in ((hp[c][2], (m + 2) % nchip), (hp[c][3], (m + 4) % nchip), (rk[c][2], m)):
            emit(src, ("wait", "r"))
            send(src, [(lo, hi, [bjob[(c, d)]], LOW8, "b")])
    for (s, d), k in sorted(ajob.items()):
        lo, hi = arange[(s, d)]
        emit(k, ("wait", "c"))
        send(k, [(lo, hi, [q for q in rk[d] if q != k], ALL16, "f")])
    for (s, d), k in sorted(bjob.items()):
        lo, hi = h45[s]
        emit(k, ("wait", "b"))
        send(k, [(lo, hi, [q for q in rk[d] if q != k], ALL16, "f")])

    for c in range(nchip):
        for q in rk[c]:
            for s in ("g", "r", "c", "b", "f"):
                if (q, s) in tot:
                    emit(q, ("wait", s))
            emit(q, ("store", 0, off[-1]))
        for q in rk[c] + hp[c]:
            if (q, "sent") in tot:
                emit(q, ("wait", "sent"))
    return prog, tot


def rank_program(g, core, T, topo):
    prog, tot = build(list(T.tables["WIDTHS"]), list(T.cores), topo)
    sems = {"sent": T.sem.sent, "g": T.sem.g, "r": T.sem.r, "c": T.sem.c, "b": T.sem.b, "f": T.sem.f}
    land = T.land
    done = set()
    nstore = 0
    for op in prog.get(core, []):
        if op[0] == "load":
            lo, hi = op[1], op[2]
            g.dma_start(land[:, lo:hi], T.x[:, 0:hi - lo]).then_inc(T.sem.loaded, 16)
            g.wait_ge(T.sem.loaded, 16)
        elif op[0] == "wait":
            if op[1] not in done:
                done.add(op[1])
                g.wait_ge(sems[op[1]], tot[(core, op[1])])
        elif op[0] == "send":
            trs = []
            for lo, hi, dsts, mask, sem in op[1]:
                ids = []
                for d in dsts:
                    rid, pid, se = topo.addr(d)
                    ids.append(bass.DstId(rid=rid, pnc=pid))
                trs.append(bass.RemoteDMATransfer(dst_ids=ids, dma_engine_mask=mask, remote_sem=sems[sem],
                                                  srcs=[land[:, lo:hi]], dsts=[land[:, lo:hi] for d in dsts]))
            g.remote_dma_fused(trs, local_sem=T.sem.sent)
        elif op[0] == "store":
            lo, hi = op[1], op[2]
            g.dma_start(T.y[:, lo:hi], land[:, lo:hi]).then_inc(T.sem.stored, 16)
            nstore += 16
    if nstore:
        g.wait_ge(T.sem.stored, nstore)
